import numpy as np
CORES = [88,96,104,112,120,216,224,232,240,248]
N = 10
R, C = 4, 256
def setup_inputs(rng):
    return {"x": rng.standard_normal((N, 128, C), dtype=np.float32), "u": rng.standard_normal((N, R, 128), dtype=np.float32), "v": rng.standard_normal((N, R, C), dtype=np.float32)}
def setup_inputs_big(rng):
    d = setup_inputs(rng)
    for k in ("u", "v"): d[k] = (d[k].astype(np.float32) * 1024.0).astype(d[k].dtype)
    for k in ("x",): d[k] = (d[k].astype(np.float32) * 1024.0 ** 2).astype(d[k].dtype)
    return d
def setup_inputs_small(rng):
    d = setup_inputs(rng)
    for k in ("u", "v"): d[k] = (d[k].astype(np.float32) * (1 / 1024.0)).astype(d[k].dtype)
    for k in ("x",): d[k] = (d[k].astype(np.float32) * (1 / 1024.0 ** 2)).astype(d[k].dtype)
    return d
def setup_inputs_apart(rng):
    d = setup_inputs(rng)
    f = (10.0 ** rng.permutation(np.linspace(-1.5, 1.5, N))).astype(np.float32).reshape(N, 1, 1)
    for k in ("u", "v"): d[k] = (d[k].astype(np.float32) * f).astype(d[k].dtype)
    for k in ("x",): d[k] = (d[k].astype(np.float32) * f * f).astype(d[k].dtype)
    return d
def reference(x, u, v):
    X, U, V = x.astype(np.float64), u.astype(np.float64), v.astype(np.float64)
    s = V.sum(axis=0)
    return {"y": np.stack([X[r] + U[r].T @ s for r in range(N)]).astype(np.float32 if x.dtype != np.float64 else np.float64)}

@@ -1,0 +1,114 @@
+from concourse.bass import DstId, RemoteDMATransfer
+from concourse.mybir import AluOpType
+
+N, R, C, P = 10, 4, 256, 128
+SIM_CORES = 256
+HELPERS, LANES = 2, 2
+
+SCRATCH = {
+    "gath": ("dram", [N, P, R * C // P], "float32"),
+    "vs": ("sbuf", [R * N, C], "float32"),
+    "us": ("sbuf", [R * N, P], "float32"),
+    "xs": ("sbuf", [P, C], "float32"),
+    "ys": ("sbuf", [P, C], "float32"),
+    "ps": ("psum", [P, C], "float32"),
+}
+SEMAPHORES = ["loaded", "relay", "near", "far", "sent", "ready", "xin", "mm", "added", "stored"]
+
+
+def _bits(mask):
+    return [e for e in range(mask.bit_length()) if (mask >> e) & 1]
+
+
+def _engines(topo, src, dsts, n):
+    common = topo.mask(src, dsts[0])
+    for d in dsts:
+        common &= topo.mask(src, d)
+    return [1 << e for e in _bits(common)[::-2][:n]]
+
+
+def _same_chip(topo, a, b):
+    return topo.host(a) == topo.host(b) and topo.chip(a) == topo.chip(b)
+
+
+def _plan(topo, cores, a):
+    i = cores.index(a)
+    others = cores[i + 1:] + cores[:i]
+    near = [b for b in others if topo.may_write(a, b)]
+    far = [b for b in others if not topo.may_write(a, b)]
+    cand = [h for h in range(SIM_CORES) if h not in cores and _same_chip(topo, h, a)
+            and all(topo.may_write(h, d) for d in far)]
+    cand.sort(key=lambda h: (topo.die(h) != topo.die(a), h))
+    helpers = cand[:HELPERS]
+    lanes = [(k, j, []) for k in range(len(helpers)) for j in range(LANES)]
+    for d in far:
+        min(lanes, key=lambda L: (L[0] + len(L[2]), -L[0], L[1]))[2].append(d)
+    shares = [[L[2] for L in lanes if L[0] == k and L[2]] for k in range(len(helpers))]
+    return near, far, helpers, shares
+
+
+def _send(g, topo, core, block, lanes, remote_sem, local_sem):
+    masks = _engines(topo, core, [d for lane in lanes for d in lane], len(lanes))
+    transfers = []
+    for lane, m in zip(lanes, masks):
+        ids = []
+        for d in lane:
+            rid, pid = topo.addr(d, core)
+            ids.append(DstId(rid=rid, pnc=pid))
+        transfers.append(RemoteDMATransfer(dst_ids=ids, dma_engine_mask=m, remote_sem=remote_sem,
+                                           srcs=[block], dsts=[block] * len(lane), alu_op=0))
+    g.remote_dma_fused(transfers, local_sem=local_sem)
+    return len(transfers)
+
+
+def rank_program(g, core, T, topo):
+    cores = list(T.cores)
+    S = T.sem
+    plane0 = [c for c in cores if c == cores[0] or topo.may_write(cores[0], c)]
+    order = plane0 + [c for c in cores if c not in plane0]
+
+    if T.rank_of(core) is None:
+        owners = [a for a in cores if _same_chip(topo, a, core)]
+        if not owners:
+            return
+        near, far, helpers, shares = _plan(topo, cores, owners[0])
+        if core not in helpers:
+            return
+        block = T.gath[order.index(owners[0])]
+        g.wait_ge(S.relay, 1)
+        n = _send(g, topo, core, block, shares[helpers.index(core)], S.far, S.sent)
+        g.wait_ge(S.sent, n)
+        return
+
+    near, far, helpers, shares = _plan(topo, cores, core)
+    slot = order.index(core)
+    block = T.gath[slot]
+    lo, hi = (0, len(plane0)) if core in plane0 else (len(plane0), N)
+    flo, fhi = (len(plane0), N) if core in plane0 else (0, len(plane0))
+
+    g.sync.dma_start(block, T.v[:]).then_inc(S.loaded, 16)
+    g.sync.dma_start(T.xs[:], T.x[:]).then_inc(S.xin, 16)
+    for k in range(N):
+        q = g.scalar if k % 5 < 3 else g.sync
+        q.dma_start(T.us[R * k:R * (k + 1), :], T.u[:]).then_inc(S.ready, 16)
+
+    g.wait_ge(S.loaded, 16)
+    n = _send(g, topo, core, block, [helpers], S.relay, S.sent) if far else 0
+    n += _send(g, topo, core, block, [near[j::LANES] for j in range(LANES) if near[j::LANES]], S.near, S.sent)
+
+    g.scalar.wait_ge(S.loaded, 16)
+    g.scalar.wait_ge(S.near, len(near))
+    g.scalar.dma_start(T.vs[R * lo:R * hi, :], T.gath[lo:hi]).then_inc(S.ready, 16)
+
+    g.sync.wait_ge(S.far, len(far))
+    g.sync.dma_start(T.vs[R * flo:R * fhi, :], T.gath[flo:fhi]).then_inc(S.ready, 16)
+
+    g.tensor.wait_ge(S.ready, 16 * (N + 2))
+    g.tensor.matmul(T.ps[:], T.us[:], T.vs[:], True, True).then_inc(S.mm, 1)
+    g.vector.wait_ge(S.xin, 16)
+    g.vector.wait_ge(S.mm, 1)
+    g.vector.tensor_tensor(T.ys[:], T.ps[:], T.xs[:], AluOpType.add).then_inc(S.added, 1)
+    g.sync.wait_ge(S.added, 1)
+    g.sync.dma_start(T.y[:], T.ys[:]).then_inc(S.stored, 16)
+    g.sync.wait_ge(S.stored, 16)
+    g.wait_ge(S.sent, n)

@@ -2,18 +2,26 @@ from concourse.bass import DstId, RemoteDMATransfer
 from concourse.mybir import AluOpType
 
 N, R, C, P = 10, 4, 256, 128
+H = C // 2
+W = 64
 SIM_CORES = 256
 HELPERS, LANES = 2, 2
 
 SCRATCH = {
-    "gath": ("dram", [N, P, R * C // P], "float32"),
-    "vs": ("sbuf", [R * N, C], "float32"),
+    "ga": ("dram", [N, P, R * H // P], "float32"),
+    "gb": ("dram", [N, P, R * H // P], "float32"),
+    "va": ("sbuf", [R * N, H], "float32"),
+    "vb": ("sbuf", [R * N, H], "float32"),
     "us": ("sbuf", [R * N, P], "float32"),
     "xs": ("sbuf", [P, C], "float32"),
     "ys": ("sbuf", [P, C], "float32"),
-    "ps": ("psum", [P, C], "float32"),
+    "ps0": ("psum", [P, 512], "float32"),
+    "ps1": ("psum", [P, 512], "float32"),
+    "ps2": ("psum", [P, 512], "float32"),
+    "ps3": ("psum", [P, 512], "float32"),
 }
-SEMAPHORES = ["loaded", "relay", "near", "far", "sent", "ready", "xin", "mm", "added", "stored"]
+SEMAPHORES = ["lda", "ldb", "rla", "rlb", "near", "fara", "farb", "sent", "ready", "xin", "fma", "fmb",
+              "mm0", "mm1", "mm2", "mm3", "ad0", "ad1", "ad2", "ad3", "sts", "stc"]
 
 
 def _bits(mask):
@@ -47,16 +55,16 @@ def _plan(topo, cores, a):
     return near, far, helpers, shares
 
 
-def _send(g, topo, core, block, lanes, remote_sem, local_sem):
-    masks = _engines(topo, core, [d for lane in lanes for d in lane], len(lanes))
+def _send(g, topo, core, parts, remote_sem, local_sem):
+    masks = _engines(topo, core, [d for _, lane in parts for d in lane], len(parts))
     transfers = []
-    for lane, m in zip(lanes, masks):
+    for (piece, lane), m in zip(parts, masks):
         ids = []
         for d in lane:
             rid, pid = topo.addr(d, core)
             ids.append(DstId(rid=rid, pnc=pid))
         transfers.append(RemoteDMATransfer(dst_ids=ids, dma_engine_mask=m, remote_sem=remote_sem,
-                                           srcs=[block], dsts=[block] * len(lane), alu_op=0))
+                                           srcs=[piece], dsts=[piece] * len(lane), alu_op=0))
     g.remote_dma_fused(transfers, local_sem=local_sem)
     return len(transfers)
 
@@ -74,41 +82,60 @@ def rank_program(g, core, T, topo):
         near, far, helpers, shares = _plan(topo, cores, owners[0])
         if core not in helpers:
             return
-        block = T.gath[order.index(owners[0])]
-        g.wait_ge(S.relay, 1)
-        n = _send(g, topo, core, block, shares[helpers.index(core)], S.far, S.sent)
+        s = order.index(owners[0])
+        mine = shares[helpers.index(core)]
+        g.wait_ge(S.rla, 1)
+        n = _send(g, topo, core, [(T.ga[s], lane) for lane in mine], S.fara, S.sent)
+        g.wait_ge(S.rlb, 1)
+        n += _send(g, topo, core, [(T.gb[s], lane) for lane in mine], S.farb, S.sent)
         g.wait_ge(S.sent, n)
         return
 
     near, far, helpers, shares = _plan(topo, cores, core)
     slot = order.index(core)
-    block = T.gath[slot]
+    a, b = T.ga[slot], T.gb[slot]
     lo, hi = (0, len(plane0)) if core in plane0 else (len(plane0), N)
     flo, fhi = (len(plane0), N) if core in plane0 else (0, len(plane0))
 
-    g.sync.dma_start(block, T.v[:]).then_inc(S.loaded, 16)
+    g.sync.dma_start(a, T.v[:, 0:H]).then_inc(S.lda, 16)
+    g.scalar.dma_start(b, T.v[:, H:C]).then_inc(S.ldb, 16)
     g.sync.dma_start(T.xs[:], T.x[:]).then_inc(S.xin, 16)
     for k in range(N):
         q = g.scalar if k % 5 < 3 else g.sync
         q.dma_start(T.us[R * k:R * (k + 1), :], T.u[:]).then_inc(S.ready, 16)
 
-    g.wait_ge(S.loaded, 16)
-    n = _send(g, topo, core, block, [helpers], S.relay, S.sent) if far else 0
-    n += _send(g, topo, core, block, [near[j::LANES] for j in range(LANES) if near[j::LANES]], S.near, S.sent)
+    g.wait_ge(S.lda, 16)
+    n = _send(g, topo, core, [(a, helpers)], S.rla, S.sent)
+    g.wait_ge(S.ldb, 16)
+    n += _send(g, topo, core, [(b, helpers)], S.rlb, S.sent)
+    n += _send(g, topo, core, [(a, near), (b, near)], S.near, S.sent)
 
-    g.scalar.wait_ge(S.loaded, 16)
-    g.scalar.wait_ge(S.near, len(near))
-    g.scalar.dma_start(T.vs[R * lo:R * hi, :], T.gath[lo:hi]).then_inc(S.ready, 16)
+    g.scalar.wait_ge(S.lda, 16)
+    g.scalar.wait_ge(S.ldb, 16)
+    g.scalar.wait_ge(S.near, 2 * len(near))
+    g.scalar.dma_start(T.va[R * lo:R * hi, :], T.ga[lo:hi]).then_inc(S.ready, 16)
+    g.scalar.dma_start(T.vb[R * lo:R * hi, :], T.gb[lo:hi]).then_inc(S.ready, 16)
 
-    g.sync.wait_ge(S.far, len(far))
-    g.sync.dma_start(T.vs[R * flo:R * fhi, :], T.gath[flo:fhi]).then_inc(S.ready, 16)
+    g.sync.wait_ge(S.fara, len(far))
+    g.sync.dma_start(T.va[R * flo:R * fhi, :], T.ga[flo:fhi]).then_inc(S.fma, 16)
+    g.sync.wait_ge(S.farb, len(far))
+    g.sync.dma_start(T.vb[R * flo:R * fhi, :], T.gb[flo:fhi]).then_inc(S.fmb, 16)
 
     g.tensor.wait_ge(S.ready, 16 * (N + 2))
-    g.tensor.matmul(T.ps[:], T.us[:], T.vs[:], True, True).then_inc(S.mm, 1)
     g.vector.wait_ge(S.xin, 16)
-    g.vector.wait_ge(S.mm, 1)
-    g.vector.tensor_tensor(T.ys[:], T.ps[:], T.xs[:], AluOpType.add).then_inc(S.added, 1)
-    g.sync.wait_ge(S.added, 1)
-    g.sync.dma_start(T.y[:], T.ys[:]).then_inc(S.stored, 16)
-    g.sync.wait_ge(S.stored, 16)
+    for i in range(C // W):
+        half, arrived = (T.va, S.fma) if i * W < H else (T.vb, S.fmb)
+        c0 = (i * W) % H
+        if c0 == 0:
+            g.tensor.wait_ge(arrived, 16)
+        ps = T["ps%d" % i]
+        g.tensor.matmul(ps[:, 0:W], T.us[:], half[:, c0:c0 + W], True, True).then_inc(S["mm%d" % i], 1)
+        g.vector.wait_ge(S["mm%d" % i], 1)
+        g.vector.tensor_tensor(T.ys[:, i * W:(i + 1) * W], ps[:, 0:W], T.xs[:, i * W:(i + 1) * W],
+                               AluOpType.add).then_inc(S["ad%d" % i], 1)
+        q, st = (g.scalar, S.stc) if i % 2 == 0 else (g.sync, S.sts)
+        q.wait_ge(S["ad%d" % i], 1)
+        q.dma_start(T.y[:, i * W:(i + 1) * W], T.ys[:, i * W:(i + 1) * W]).then_inc(st, 16)
+    g.scalar.wait_ge(S.stc, 32)
+    g.sync.wait_ge(S.sts, 32)
     g.wait_ge(S.sent, n)

from concourse.bass import DstId, RemoteDMATransfer
from concourse.mybir import AluOpType

N, R, C, P = 10, 4, 256, 128
H = C // 2
W = 64
SIM_CORES = 256
HELPERS, LANES = 2, 2

SCRATCH = {
    "ga": ("dram", [N, P, R * H // P], "float32"),
    "gb": ("dram", [N, P, R * H // P], "float32"),
    "va": ("sbuf", [R * N, H], "float32"),
    "vb": ("sbuf", [R * N, H], "float32"),
    "us": ("sbuf", [R * N, P], "float32"),
    "xs": ("sbuf", [P, C], "float32"),
    "ys": ("sbuf", [P, C], "float32"),
    "ps0": ("psum", [P, 512], "float32"),
    "ps1": ("psum", [P, 512], "float32"),
    "ps2": ("psum", [P, 512], "float32"),
    "ps3": ("psum", [P, 512], "float32"),
}
SEMAPHORES = ["lda", "ldb", "rla", "rlb", "near", "fara", "farb", "sent", "ready", "xin", "fma", "fmb",
              "mm0", "mm1", "mm2", "mm3", "ad0", "ad1", "ad2", "ad3", "sts", "stc"]


def _bits(mask):
    return [e for e in range(mask.bit_length()) if (mask >> e) & 1]


def _engines(topo, src, dsts, n):
    common = topo.mask(src, dsts[0])
    for d in dsts:
        common &= topo.mask(src, d)
    return [1 << e for e in _bits(common)[::-2][:n]]


def _same_chip(topo, a, b):
    return topo.host(a) == topo.host(b) and topo.chip(a) == topo.chip(b)


def _plan(topo, cores, a):
    i = cores.index(a)
    others = cores[i + 1:] + cores[:i]
    near = [b for b in others if topo.may_write(a, b)]
    far = [b for b in others if not topo.may_write(a, b)]
    cand = [h for h in range(SIM_CORES) if h not in cores and _same_chip(topo, h, a)
            and all(topo.may_write(h, d) for d in far)]
    cand.sort(key=lambda h: (topo.die(h) != topo.die(a), h))
    helpers = cand[:HELPERS]
    lanes = [(k, j, []) for k in range(len(helpers)) for j in range(LANES)]
    for d in far:
        min(lanes, key=lambda L: (L[0] + len(L[2]), -L[0], L[1]))[2].append(d)
    shares = [[L[2] for L in lanes if L[0] == k and L[2]] for k in range(len(helpers))]
    return near, far, helpers, shares


def _send(g, topo, core, parts, remote_sem, local_sem):
    masks = _engines(topo, core, [d for _, lane in parts for d in lane], len(parts))
    transfers = []
    for (piece, lane), m in zip(parts, masks):
        ids = []
        for d in lane:
            rid, pid = topo.addr(d, core)
            ids.append(DstId(rid=rid, pnc=pid))
        transfers.append(RemoteDMATransfer(dst_ids=ids, dma_engine_mask=m, remote_sem=remote_sem,
                                           srcs=[piece], dsts=[piece] * len(lane), alu_op=0))
    g.remote_dma_fused(transfers, local_sem=local_sem)
    return len(transfers)


def rank_program(g, core, T, topo):
    cores = list(T.cores)
    S = T.sem
    plane0 = [c for c in cores if c == cores[0] or topo.may_write(cores[0], c)]
    order = plane0 + [c for c in cores if c not in plane0]

    if T.rank_of(core) is None:
        owners = [a for a in cores if _same_chip(topo, a, core)]
        if not owners:
            return
        near, far, helpers, shares = _plan(topo, cores, owners[0])
        if core not in helpers:
            return
        s = order.index(owners[0])
        mine = shares[helpers.index(core)]
        g.wait_ge(S.rla, 1)
        n = _send(g, topo, core, [(T.ga[s], lane) for lane in mine], S.fara, S.sent)
        g.wait_ge(S.rlb, 1)
        n += _send(g, topo, core, [(T.gb[s], lane) for lane in mine], S.farb, S.sent)
        g.wait_ge(S.sent, n)
        return

    near, far, helpers, shares = _plan(topo, cores, core)
    slot = order.index(core)
    a, b = T.ga[slot], T.gb[slot]
    lo, hi = (0, len(plane0)) if core in plane0 else (len(plane0), N)
    flo, fhi = (len(plane0), N) if core in plane0 else (0, len(plane0))

    g.sync.dma_start(a, T.v[:, 0:H]).then_inc(S.lda, 16)
    g.scalar.dma_start(b, T.v[:, H:C]).then_inc(S.ldb, 16)
    g.sync.dma_start(T.xs[:], T.x[:]).then_inc(S.xin, 16)
    for k in range(N):
        q = g.scalar if k % 5 < 3 else g.sync
        q.dma_start(T.us[R * k:R * (k + 1), :], T.u[:]).then_inc(S.ready, 16)

    g.wait_ge(S.lda, 16)
    n = _send(g, topo, core, [(a, helpers)], S.rla, S.sent)
    g.wait_ge(S.ldb, 16)
    n += _send(g, topo, core, [(b, helpers)], S.rlb, S.sent)
    n += _send(g, topo, core, [(a, near), (b, near)], S.near, S.sent)

    g.scalar.wait_ge(S.lda, 16)
    g.scalar.wait_ge(S.ldb, 16)
    g.scalar.wait_ge(S.near, 2 * len(near))
    g.scalar.dma_start(T.va[R * lo:R * hi, :], T.ga[lo:hi]).then_inc(S.ready, 16)
    g.scalar.dma_start(T.vb[R * lo:R * hi, :], T.gb[lo:hi]).then_inc(S.ready, 16)

    g.sync.wait_ge(S.fara, len(far))
    g.sync.dma_start(T.va[R * flo:R * fhi, :], T.ga[flo:fhi]).then_inc(S.fma, 16)
    g.sync.wait_ge(S.farb, len(far))
    g.sync.dma_start(T.vb[R * flo:R * fhi, :], T.gb[flo:fhi]).then_inc(S.fmb, 16)

    g.tensor.wait_ge(S.ready, 16 * (N + 2))
    g.vector.wait_ge(S.xin, 16)
    for i in range(C // W):
        half, arrived = (T.va, S.fma) if i * W < H else (T.vb, S.fmb)
        c0 = (i * W) % H
        if c0 == 0:
            g.tensor.wait_ge(arrived, 16)
        ps = T["ps%d" % i]
        g.tensor.matmul(ps[:, 0:W], T.us[:], half[:, c0:c0 + W], True, True).then_inc(S["mm%d" % i], 1)
        g.vector.wait_ge(S["mm%d" % i], 1)
        g.vector.tensor_tensor(T.ys[:, i * W:(i + 1) * W], ps[:, 0:W], T.xs[:, i * W:(i + 1) * W],
                               AluOpType.add).then_inc(S["ad%d" % i], 1)
        q, st = (g.scalar, S.stc) if i % 2 == 0 else (g.sync, S.sts)
        q.wait_ge(S["ad%d" % i], 1)
        q.dma_start(T.y[:, i * W:(i + 1) * W], T.ys[:, i * W:(i + 1) * W]).then_inc(st, 16)
    g.scalar.wait_ge(S.stc, 32)
    g.sync.wait_ge(S.sts, 32)
    g.wait_ge(S.sent, n)
